import numpy as np, ml_dtypes
CORES = [3,11,19,27,35,43]
N = 6
import mx_ref
BF = ml_dtypes.bfloat16
def entries(a):
    return np.ascontiguousarray(a.T).reshape(-1)
def table(e):
    return np.ascontiguousarray(np.reshape(e, (-1, 16)).T).astype(np.int32)
def gentries(a):
    return np.ascontiguousarray(a.reshape(8, 16, -1).transpose(0, 2, 1)).reshape(8, -1)
def gtable(e):
    e = np.asarray(e); return np.ascontiguousarray(e.reshape(8, -1, 16).transpose(0, 2, 1)).reshape(128, -1).astype(np.int32)
def cols(t, e):
    v = np.concatenate([t.reshape(128, -1, 4), np.zeros((128, 1, 4), BF)], axis=1)
    return np.ascontiguousarray(v[:, e]).reshape(128, -1)
def gcols(t, e):
    v = np.concatenate([t.reshape(8, 16, -1, 4), np.zeros((8, 16, 1, 4), BF)], axis=2)
    return np.ascontiguousarray(np.stack([v[g][:, e[g]] for g in range(8)])).reshape(128, -1)
def cut(t, i, w=512):
    return t[:, w * i:w * i + w]
def f(rng, *shape):
    return mx_ref.flush((rng.standard_normal(shape, dtype=np.float32) * np.exp2(rng.integers(-2, 3, shape[:-1] + (1,)))).astype(BF))
def wide(rng, *shape, cols=0):
    v = rng.standard_normal(shape, dtype=np.float32) * np.exp2(rng.integers(-12, 13, shape)).astype(np.float32)
    if cols: v *= np.repeat(np.exp2(rng.integers(-cols, cols + 1, shape[:-2] + (1, shape[-1] // 4))) * (rng.random(shape[:-2] + (1, shape[-1] // 4)) > 0.0625), 4, axis=-1).astype(np.float32)
    return mx_ref.flush(v.astype(BF))
T, CAPP, S, O = 256, 96, 512, 2
def lists(rng, kind=""):
    sn = np.full((N, N, CAPP), -1)
    for s in range(N):
        for d in range(N):
            n = CAPP if kind == "foreign" else 0 if kind == "own" else int(rng.integers(0, CAPP + 1))
            if d != s: sn[s, d, rng.permutation(CAPP)[:n]] = rng.integers(0, T, n)
    if kind == "one":
        s, d = rng.permutation(N)[:2]; sn[s, d] = rng.integers(0, T)
    ql = []
    for r in range(N):
        slots = T + np.flatnonzero(sn[:, r].reshape(-1) >= 0)
        if kind == "foreign": e = rng.permutation(np.resize(slots, 4 * S)).reshape(4, S)
        elif kind == "own": e = rng.integers(0, T, (4, S))
        else: e = rng.choice(np.concatenate([np.arange(T), slots]), (4, S))
        if kind == "whole": e = np.repeat(e[:1], 4, axis=0)
        if kind == "one":
            for u in rng.permutation(4)[:int(rng.integers(1, 5))]: e[u] = e[u, 0]
        ql.append(gtable(np.repeat(e, 2, axis=0)))
    return {"sn": np.stack([table(sn[s].reshape(-1)) for s in range(N)]), "ql": np.stack(ql)}
def setup_inputs(rng):
    return {"x": f(rng, N, 128, 4 * T), "w": f(rng, N, 128, O * 512), **lists(rng)}
def setup_inputs_whole(rng):
    return {**setup_inputs(rng), **lists(rng, "whole")}
def setup_inputs_foreign(rng):
    return {**setup_inputs(rng), **lists(rng, "foreign")}
def setup_inputs_own(rng):
    return {**setup_inputs(rng), **lists(rng, "own")}
def setup_inputs_one(rng):
    return {**setup_inputs(rng), **lists(rng, "one")}
def setup_inputs_spread(rng):
    d = setup_inputs(rng); d["x"] = wide(rng, N, 128, 4 * T, cols=8); return d
def check_inputs(d):
    b = []; to = [entries(d["sn"][s]).reshape(N, CAPP) for s in range(N)]
    for r in range(N):
        if to[r].min() < -1 or to[r].max() >= T or (to[r][r] != -1).any(): b.append("sn")
        e = gentries(d["ql"][r]); there = np.concatenate([np.ones(T, bool)] + [to[s][r] >= 0 for s in range(N)])
        if e.min() < 0 or e.max() >= T + N * CAPP or not there[np.clip(e, 0, T + N * CAPP - 1)].all() or (e[0::2] != e[1::2]).any(): b.append("ql")
    return b
def reference(x, w, sn, ql):
    to = [entries(sn[s]).reshape(N, CAPP) for s in range(N)]
    y = np.zeros((N, 128, O * S), np.float32)
    for r in range(N):
        have = np.concatenate([x[r]] + [cols(x[s], to[s][r]) for s in range(N)], axis=1)
        V = mx_ref.quantize(gcols(have, gentries(ql[r])))
        for o in range(O): y[r][:, S * o:S * o + S] = mx_ref.matmul(mx_ref.quantize(np.ascontiguousarray(cut(w[r], o))), V)
    return {"y": y}

@@ -1,0 +1,184 @@
+from concourse.bass import DstId, RemoteDMATransfer
+from concourse.mybir import dt, ActivationFunctionType
+
+N = 6
+XC, CAPP, S, O = 256, 96, 512, 2
+PIECES = [(128, "vv"), (192, "vs"), (192, "vs")]
+K = CAPP // 16
+HV = XC + N * CAPP
+
+SCRATCH = {
+    "xt": ("sbuf", [128, 4 * XC], "bfloat16"),
+    "wt": ("sbuf", [128, O * 512], "bfloat16"),
+    "snt": ("sbuf", [128, N * K], "int32"),
+    "qlt": ("sbuf", [128, S // 16], "int32"),
+    "offs": ("sbuf", [128, N * K], "uint16"),
+    "offv": ("sbuf", [128, S // 16], "uint16"),
+    "qx": ("sbuf", [128, XC], "float8_e4m3fn_x4"),
+    "sx": ("sbuf", [128, XC], "uint8"),
+    "qw": ("sbuf", [128, O * 128], "float8_e4m3fn_x4"),
+    "sw": ("sbuf", [128, O * 128], "uint8"),
+    "qs": ("sbuf", [128, N * CAPP], "float8_e4m3fn_x4"),
+    "ss": ("sbuf", [128, N * CAPP], "uint8"),
+    "have": ("sbuf", [128, HV], "float8_e4m3fn_x4"),
+    "haves": ("sbuf", [128, HV], "uint8"),
+    "qv": ("sbuf", [128, S], "float8_e4m3fn_x4"),
+    "sv": ("sbuf", [128, S], "uint8"),
+    "yt": ("sbuf", [128, O * S], "float32"),
+    "acc": ("psum", [128, 512 * O * len(PIECES)], "float32"),
+}
+SEMAPHORES = ["ldx", "ldsn", "ldql", "ldw", "offs", "qx", "have", "qw", "offv", "pc0", "pc1", "ps0", "ps1",
+              "arrc", "arrs", "sent", "sty"] + \
+             ["vc%d" % i for i in range(len(PIECES))] + ["vs%d" % i for i in range(len(PIECES))] + \
+             ["mm%d" % i for i in range(O * len(PIECES))] + ["cp%d" % i for i in range(O * len(PIECES))]
+
+
+def bits(engines):
+    m = 0
+    for e in engines:
+        m |= 1 << e
+    return m
+
+
+def roads(src, T, topo):
+    c = T.cores[src]
+    first = (src + N // 2) % N
+    rest = [(src + k) % N for k in range(1, N) if (src + k) % N != first]
+    e0 = topo.engines(c, T.cores[first])
+    fused = []
+    for i, d in enumerate(rest):
+        e = topo.engines(c, T.cores[d])
+        w = len(e) // len(rest)
+        fused.append((d, e[w * i:w * i + w]))
+    return (first, e0), fused
+
+
+def runs(ranks):
+    out = []
+    for d in sorted(ranks):
+        if out and out[-1][1] == d:
+            out[-1] = (out[-1][0], d + 1)
+        else:
+            out.append((d, d + 1))
+    return out
+
+
+def rank_program(g, core, T, topo):
+    r = T.rank_of(core)
+    if r is None:
+        return
+    sem = T.sem
+    COPY = ActivationFunctionType.Copy
+    (m, me), fused = roads(r, T, topo)
+    rest = runs([d for d, _ in fused])
+
+    g.sync.dma_start(T.xt[:], T.x[:]).then_inc(sem.ldx, 16)
+    for k in range(8):
+        q = g.sync if k % 2 else g.scalar
+        q.dma_start(T.snt[16 * k:16 * k + 16, :], T.sn[:]).then_inc(sem.ldsn, 16)
+    g.sync.dma_start(T.wt[:], T.w[:]).then_inc(sem.ldw, 16)
+    g.sync.dma_start(T.qlt[:], T.ql[:]).then_inc(sem.ldql, 16)
+
+    def slots(d0, d1):
+        return slice(CAPP * d0, CAPP * d1), slice(K * d0, K * d1)
+
+    v = g.vector
+    v.wait_ge(sem.ldx, 16)
+    v.quantize_mx(T.qx[:], T.sx[:], T.xt[:]).then_inc(sem.qx, 1)
+    v.wait_ge(sem.ldsn, 128)
+    v.tensor_copy(T.offs[:], T.snt[:]).then_inc(sem.offs, 1)
+    v.wait_ge(sem.qx, 1)
+    v.wait_ge(sem.offs, 1)
+    for name, todo in (("pc0", [(m, m + 1)]), ("pc1", rest)):
+        for a, b in todo:
+            c, o = slots(a, b)
+            v.tensor_copy(T.qs[:, c].bitcast(dt.uint32),
+                          T.qx[:].bitcast(dt.uint32).indirect(T.offs[:, o])).then_inc(sem[name], 1)
+    v.quantize_mx(T.have[:, 0:XC], T.haves[:, 0:XC], T.xt[:]).then_inc(sem.have, 1)
+    v.wait_ge(sem.ldw, 16)
+    v.quantize_mx(T.qw[:], T.sw[:], T.wt[:]).then_inc(sem.qw, 1)
+    v.wait_ge(sem.ldql, 16)
+    v.tensor_copy(T.offv[:], T.qlt[:]).then_inc(sem.offv, 1)
+
+    s = g.scalar
+    s.wait_ge(sem.qx, 1)
+    s.wait_ge(sem.offs, 1)
+    for name, todo in (("ps0", [(m, m + 1)]), ("ps1", rest)):
+        for a, b in todo:
+            c, o = slots(a, b)
+            s.activation(T.ss[:, c], T.sx[:].indirect(T.offs[:, o]), COPY).then_inc(sem[name], 1)
+
+    here = slice(XC + CAPP * r, XC + CAPP * r + CAPP)
+
+    def ends(d, scales):
+        c = slice(CAPP * d, CAPP * d + CAPP)
+        if scales:
+            return T.haves[:, here], T.ss[:, c], sem.arrs
+        return T.have[:, here].bitcast(dt.uint8), T.qs[:, c].bitcast(dt.uint8), sem.arrc
+
+    def single(scales):
+        out, src, arr = ends(m, scales)
+        rid, pid, _ = topo.addr(T.cores[m])
+        g.remote_dma(out, src, arr, sem.sent, pid, rid, bits(me))
+
+    def four(scales):
+        ts = []
+        for d, e in fused:
+            out, src, arr = ends(d, scales)
+            rid, pid, _ = topo.addr(T.cores[d])
+            ts.append(RemoteDMATransfer(dst_ids=[DstId(rid=rid, pnc=pid)], dma_engine_mask=bits(e),
+                                        remote_sem=arr, srcs=[src], dsts=[out]))
+        g.remote_dma_fused(ts, local_sem=sem.sent)
+
+    g.wait_ge(sem.pc0, 1)
+    single(False)
+    g.wait_ge(sem.pc1, len(rest))
+    four(False)
+    g.wait_ge(sem.ps1, len(rest))
+    four(True)
+    g.wait_ge(sem.ps0, 1)
+    single(True)
+    g.wait_ge(sem.sent, 2 * (len(me) + sum(len(e) for _, e in fused)))
+
+    come = 0
+    for q in range(N):
+        if q != r:
+            (f, fe), fs = roads(q, T, topo)
+            come += sum(len(e) for d, e in [(f, fe)] + fs if d == r)
+
+    ends_at = [sum(p[0] for p in PIECES[:i + 1]) for i in range(len(PIECES))]
+    cols = [(e - p[0], e) for e, p in zip(ends_at, PIECES)]
+    v.wait_ge(sem.offv, 1)
+    v.wait_ge(sem.have, 1)
+    v.wait_ge(sem.arrc, come)
+    for i, (a, b) in enumerate(cols):
+        v.tensor_copy(T.qv[:, a:b].bitcast(dt.uint32),
+                      T.have[:].bitcast(dt.uint32).indirect(T.offv[:, a // 16:b // 16])).then_inc(sem["vc%d" % i], 1)
+    s.wait_ge(sem.offv, 1)
+    s.wait_ge(sem.have, 1)
+    s.wait_ge(sem.arrs, come)
+    t = g.tensor
+    t.wait_ge(sem.qw, 1)
+    for i, (a, b) in enumerate(cols):
+        s.activation(T.sv[:, a:b], T.haves[:].indirect(T.offv[:, a // 16:b // 16]), COPY).then_inc(sem["vs%d" % i], 1)
+        t.wait_ge(sem["vc%d" % i], 1)
+        t.wait_ge(sem["vs%d" % i], 1)
+        for o in range(O):
+            k = O * i + o
+            t.matmul_mx(T.acc[:, 512 * k:512 * k + b - a], T.qw[:, 128 * o:128 * o + 128],
+                        T.sw[:, 128 * o:128 * o + 128], T.qv[:, a:b], T.sv[:, a:b],
+                        True, True).then_inc(sem["mm%d" % k], 1)
+
+    for i, (a, b) in enumerate(cols):
+        for o in range(O):
+            k = O * i + o
+            src, dst = T.acc[:, 512 * k:512 * k + b - a], slice(S * o + a, S * o + b)
+            if PIECES[i][1][o] == "v":
+                v.wait_ge(sem["mm%d" % k], 1)
+                v.tensor_copy(T.yt[:, dst], src).then_inc(sem["cp%d" % k], 1)
+            else:
+                s.wait_ge(sem["mm%d" % k], 1)
+                s.activation(T.yt[:, dst], src, COPY).then_inc(sem["cp%d" % k], 1)
+            g.sync.wait_ge(sem["cp%d" % k], 1)
+            g.sync.dma_start(T.y[:, dst], T.yt[:, dst]).then_inc(sem.sty, 16)
+    g.sync.wait_ge(sem.sty, 16 * O * len(PIECES))

@@ -3,9 +3,15 @@ from concourse.mybir import dt, ActivationFunctionType
 
 N = 6
 XC, CAPP, S, O = 256, 96, 512, 2
-PIECES = [(128, "vv"), (192, "vs"), (192, "vs")]
 K = CAPP // 16
+SPLIT = 4
+HALF = XC // 2
 HV = XC + N * CAPP
+
+PIECES = [128, 192, 192]
+VECTOR = [("c", 0), ("c", 1), ("c", 2), ("y", 1, 1), ("y", 2, 0)]
+SCALAR = [("s", 0), ("s", 1), ("s", 2), ("y", 0, 0), ("y", 0, 1), ("y", 1, 0), ("y", 2, 1)]
+P = len(PIECES)
 
 SCRATCH = {
     "xt": ("sbuf", [128, 4 * XC], "bfloat16"),
@@ -25,12 +31,13 @@ SCRATCH = {
     "qv": ("sbuf", [128, S], "float8_e4m3fn_x4"),
     "sv": ("sbuf", [128, S], "uint8"),
     "yt": ("sbuf", [128, O * S], "float32"),
-    "acc": ("psum", [128, 512 * O * len(PIECES)], "float32"),
+    "acc": ("psum", [128, 512 * O * P], "float32"),
 }
-SEMAPHORES = ["ldx", "ldsn", "ldql", "ldw", "offs", "qx", "have", "qw", "offv", "pc0", "pc1", "ps0", "ps1",
+SEMAPHORES = ["ldx0", "ldx1", "ldsn", "ldql", "ldw", "offs", "qx", "have", "qw", "offv",
               "arrc", "arrs", "sent", "sty"] + \
-             ["vc%d" % i for i in range(len(PIECES))] + ["vs%d" % i for i in range(len(PIECES))] + \
-             ["mm%d" % i for i in range(O * len(PIECES))] + ["cp%d" % i for i in range(O * len(PIECES))]
+             ["pc%d" % i for i in range(N)] + ["ps%d" % i for i in range(N)] + \
+             ["c%d" % i for i in range(P)] + ["s%d" % i for i in range(P)] + \
+             ["mm%d" % i for i in range(O * P)] + ["y%d" % i for i in range(O * P)]
 
 
 def bits(engines):
@@ -40,27 +47,25 @@ def bits(engines):
     return m
 
 
-def roads(src, T, topo):
-    c = T.cores[src]
-    first = (src + N // 2) % N
-    rest = [(src + k) % N for k in range(1, N) if (src + k) % N != first]
-    e0 = topo.engines(c, T.cores[first])
-    fused = []
-    for i, d in enumerate(rest):
-        e = topo.engines(c, T.cores[d])
-        w = len(e) // len(rest)
-        fused.append((d, e[w * i:w * i + w]))
-    return (first, e0), fused
+def near(r, T, topo):
+    chip = lambda d: topo.chip(T.cores[d])
+    mate = [d for d in range(N) if topo.mates(chip(r), chip(d))][0]
+    plane = [d for d in range(N) if d == r or topo.same_plane(chip(r), chip(d))]
+    i = plane.index(r)
+    return mate, plane[i - 1], plane[(i + 1) % len(plane)]
 
 
-def runs(ranks):
-    out = []
-    for d in sorted(ranks):
-        if out and out[-1][1] == d:
-            out[-1] = (out[-1][0], d + 1)
-        else:
-            out.append((d, d + 1))
-    return out
+def calls(r, T, topo):
+    mate, prev, nxt = near(r, T, topo)
+    far = [near(d, T, topo)[0] for d in (prev, nxt)]
+    e = topo.engines(T.cores[r], T.cores[mate])
+    two = lambda ds: [(d, e[i::2]) for i, d in enumerate(ds)]
+    return [("s", two(far)[:1]), ("s", two(far)[1:]), ("s", two([prev, nxt])),
+            ("c", two(far)), ("c", two([prev, nxt])), ("s", [(mate, e)]), ("c", [(mate, e)])]
+
+
+def run(a):
+    return slice(CAPP * a, CAPP * a + CAPP)
 
 
 def rank_program(g, core, T, topo):
@@ -69,116 +74,112 @@ def rank_program(g, core, T, topo):
         return
     sem = T.sem
     COPY = ActivationFunctionType.Copy
-    (m, me), fused = roads(r, T, topo)
-    rest = runs([d for d, _ in fused])
+    plan = calls(r, T, topo)
 
-    g.sync.dma_start(T.xt[:], T.x[:]).then_inc(sem.ldx, 16)
-    for k in range(8):
-        q = g.sync if k % 2 else g.scalar
-        q.dma_start(T.snt[16 * k:16 * k + 16, :], T.sn[:]).then_inc(sem.ldsn, 16)
-    g.sync.dma_start(T.wt[:], T.w[:]).then_inc(sem.ldw, 16)
+    g.sync.dma_start(T.xt[:, 0:4 * HALF], T.x[:, 0:4 * HALF]).then_inc(sem.ldx0, 16)
+    g.scalar.dma_start(T.snt[0:16, :], T.sn[:]).then_inc(sem.ldsn, 16)
+    g.sync.dma_start(T.snt[16:32, :], T.sn[:]).then_inc(sem.ldsn, 16)
+    g.sync.dma_start(T.xt[:, 4 * HALF:], T.x[:, 4 * HALF:]).then_inc(sem.ldx1, 16)
     g.sync.dma_start(T.qlt[:], T.ql[:]).then_inc(sem.ldql, 16)
+    g.sync.dma_start(T.wt[:], T.w[:]).then_inc(sem.ldw, 16)
 
-    def slots(d0, d1):
-        return slice(CAPP * d0, CAPP * d1), slice(K * d0, K * d1)
+    scales = [d for kind, to in plan if kind == "s" for d, _ in to]
+    first = scales[0]
 
-    v = g.vector
-    v.wait_ge(sem.ldx, 16)
-    v.quantize_mx(T.qx[:], T.sx[:], T.xt[:]).then_inc(sem.qx, 1)
-    v.wait_ge(sem.ldsn, 128)
-    v.tensor_copy(T.offs[:], T.snt[:]).then_inc(sem.offs, 1)
-    v.wait_ge(sem.qx, 1)
-    v.wait_ge(sem.offs, 1)
-    for name, todo in (("pc0", [(m, m + 1)]), ("pc1", rest)):
-        for a, b in todo:
-            c, o = slots(a, b)
+    def parts(d):
+        cuts = (0, SPLIT, K) if d == first else (0, K)
+        return [(slice(CAPP * d + 16 * a, CAPP * d + 16 * b), T.offs[:, K * d + a:K * d + b])
+                for a, b in zip(cuts, cuts[1:])]
+
+    v, s = g.vector, g.scalar
+    v.wait_ge(sem.ldx0, 16)
+    v.quantize_mx(T.qx[:, 0:HALF], T.sx[:, 0:HALF], T.xt[:, 0:4 * HALF]).then_inc(sem.qx, 1)
+    v.wait_ge(sem.ldsn, 32)
+    for u in range(4):
+        v.tensor_copy(T.offs[32 * u:32 * u + 32, :], T.snt[0:32, :]).then_inc(sem.offs, 1)
+    v.wait_ge(sem.ldx1, 16)
+    v.quantize_mx(T.qx[:, HALF:], T.sx[:, HALF:], T.xt[:, 4 * HALF:]).then_inc(sem.qx, 1)
+    v.wait_ge(sem.offs, 4)
+    v.wait_ge(sem.qx, 2)
+    c, o = parts(first)[0]
+    v.tensor_copy(T.ss[:, c], T.sx[:].indirect(o)).then_inc(sem["ps%d" % first], 1)
+    for d in [d for kind, to in plan if kind == "c" for d, _ in to]:
+        for c, o in parts(d):
             v.tensor_copy(T.qs[:, c].bitcast(dt.uint32),
-                          T.qx[:].bitcast(dt.uint32).indirect(T.offs[:, o])).then_inc(sem[name], 1)
+                          T.qx[:].bitcast(dt.uint32).indirect(o)).then_inc(sem["pc%d" % d], 1)
     v.quantize_mx(T.have[:, 0:XC], T.haves[:, 0:XC], T.xt[:]).then_inc(sem.have, 1)
-    v.wait_ge(sem.ldw, 16)
-    v.quantize_mx(T.qw[:], T.sw[:], T.wt[:]).then_inc(sem.qw, 1)
     v.wait_ge(sem.ldql, 16)
     v.tensor_copy(T.offv[:], T.qlt[:]).then_inc(sem.offv, 1)
+    v.wait_ge(sem.ldw, 16)
+    v.quantize_mx(T.qw[:], T.sw[:], T.wt[:]).then_inc(sem.qw, 1)
 
-    s = g.scalar
-    s.wait_ge(sem.qx, 1)
-    s.wait_ge(sem.offs, 1)
-    for name, todo in (("ps0", [(m, m + 1)]), ("ps1", rest)):
-        for a, b in todo:
-            c, o = slots(a, b)
-            s.activation(T.ss[:, c], T.sx[:].indirect(T.offs[:, o]), COPY).then_inc(sem[name], 1)
+    s.wait_ge(sem.offs, 4)
+    s.wait_ge(sem.qx, 2)
+    for d in scales:
+        c, o = parts(d)[-1]
+        s.activation(T.ss[:, c], T.sx[:].indirect(o), COPY).then_inc(sem["ps%d" % d], 1)
 
     here = slice(XC + CAPP * r, XC + CAPP * r + CAPP)
-
-    def ends(d, scales):
-        c = slice(CAPP * d, CAPP * d + CAPP)
-        if scales:
-            return T.haves[:, here], T.ss[:, c], sem.arrs
-        return T.have[:, here].bitcast(dt.uint8), T.qs[:, c].bitcast(dt.uint8), sem.arrc
-
-    def single(scales):
-        out, src, arr = ends(m, scales)
-        rid, pid, _ = topo.addr(T.cores[m])
-        g.remote_dma(out, src, arr, sem.sent, pid, rid, bits(me))
-
-    def four(scales):
+    for kind, to in plan:
         ts = []
-        for d, e in fused:
-            out, src, arr = ends(d, scales)
+        for d, e in to:
+            g.wait_ge(sem["p%s%d" % (kind, d)], len(parts(d)))
+            if kind == "s":
+                out, src, arr = T.haves[:, here], T.ss[:, run(d)], sem.arrs
+            else:
+                out, src, arr = T.have[:, here].bitcast(dt.uint8), T.qs[:, run(d)].bitcast(dt.uint8), sem.arrc
             rid, pid, _ = topo.addr(T.cores[d])
+            if len(to) == 1:
+                g.remote_dma(out, src, arr, sem.sent, pid, rid, bits(e))
             ts.append(RemoteDMATransfer(dst_ids=[DstId(rid=rid, pnc=pid)], dma_engine_mask=bits(e),
                                         remote_sem=arr, srcs=[src], dsts=[out]))
-        g.remote_dma_fused(ts, local_sem=sem.sent)
+        if len(to) > 1:
+            g.remote_dma_fused(ts, local_sem=sem.sent)
+    g.wait_ge(sem.sent, sum(len(e) for _, to in plan for _, e in to))
+    come = {k: sum(len(e) for q in range(N) for kind, to in calls(q, T, topo) for d, e in to if kind == k and d == r)
+            for k in "cs"}
 
-    g.wait_ge(sem.pc0, 1)
-    single(False)
-    g.wait_ge(sem.pc1, len(rest))
-    four(False)
-    g.wait_ge(sem.ps1, len(rest))
-    four(True)
-    g.wait_ge(sem.ps0, 1)
-    single(True)
-    g.wait_ge(sem.sent, 2 * (len(me) + sum(len(e) for _, e in fused)))
+    cols = [(sum(PIECES[:i]), sum(PIECES[:i + 1])) for i in range(P)]
+    for q, todo in ((v, VECTOR), (s, SCALAR)):
+        q.wait_ge(sem.offv, 1)
+        q.wait_ge(sem.have, 1)
+        seen = set()
+        for step in todo:
+            kind, i = step[0], step[1]
+            a, b = cols[i]
+            o = T.offv[:, a // 16:b // 16]
+            if kind == "c":
+                if kind not in seen:
+                    q.wait_ge(sem.arrc, come["c"])
+                v.tensor_copy(T.qv[:, a:b].bitcast(dt.uint32),
+                              T.have[:].bitcast(dt.uint32).indirect(o)).then_inc(sem["c%d" % i], 1)
+            elif kind == "s":
+                if kind not in seen:
+                    q.wait_ge(sem.arrs, come["s"])
+                if q is v:
+                    call = v.tensor_copy(T.sv[:, a:b], T.haves[:].indirect(o))
+                else:
+                    call = s.activation(T.sv[:, a:b], T.haves[:].indirect(o), COPY)
+                call.then_inc(sem["s%d" % i], 1)
+            else:
+                k = O * i + step[2]
+                src, dst = T.acc[:, 512 * k:512 * k + b - a], T.yt[:, S * step[2] + a:S * step[2] + b]
+                q.wait_ge(sem["mm%d" % k], 1)
+                call = v.tensor_copy(dst, src) if q is v else s.activation(dst, src, COPY)
+                call.then_inc(sem["y%d" % k], 1)
+            seen.add(kind)
 
-    come = 0
-    for q in range(N):
-        if q != r:
-            (f, fe), fs = roads(q, T, topo)
-            come += sum(len(e) for d, e in [(f, fe)] + fs if d == r)
-
-    ends_at = [sum(p[0] for p in PIECES[:i + 1]) for i in range(len(PIECES))]
-    cols = [(e - p[0], e) for e, p in zip(ends_at, PIECES)]
-    v.wait_ge(sem.offv, 1)
-    v.wait_ge(sem.have, 1)
-    v.wait_ge(sem.arrc, come)
-    for i, (a, b) in enumerate(cols):
-        v.tensor_copy(T.qv[:, a:b].bitcast(dt.uint32),
-                      T.have[:].bitcast(dt.uint32).indirect(T.offv[:, a // 16:b // 16])).then_inc(sem["vc%d" % i], 1)
-    s.wait_ge(sem.offv, 1)
-    s.wait_ge(sem.have, 1)
-    s.wait_ge(sem.arrs, come)
     t = g.tensor
     t.wait_ge(sem.qw, 1)
     for i, (a, b) in enumerate(cols):
-        s.activation(T.sv[:, a:b], T.haves[:].indirect(T.offv[:, a // 16:b // 16]), COPY).then_inc(sem["vs%d" % i], 1)
-        t.wait_ge(sem["vc%d" % i], 1)
-        t.wait_ge(sem["vs%d" % i], 1)
+        t.wait_ge(sem["c%d" % i], 1)
+        t.wait_ge(sem["s%d" % i], 1)
         for o in range(O):
             k = O * i + o
             t.matmul_mx(T.acc[:, 512 * k:512 * k + b - a], T.qw[:, 128 * o:128 * o + 128],
                         T.sw[:, 128 * o:128 * o + 128], T.qv[:, a:b], T.sv[:, a:b],
                         True, True).then_inc(sem["mm%d" % k], 1)
-
-    for i, (a, b) in enumerate(cols):
-        for o in range(O):
-            k = O * i + o
-            src, dst = T.acc[:, 512 * k:512 * k + b - a], slice(S * o + a, S * o + b)
-            if PIECES[i][1][o] == "v":
-                v.wait_ge(sem["mm%d" % k], 1)
-                v.tensor_copy(T.yt[:, dst], src).then_inc(sem["cp%d" % k], 1)
-            else:
-                s.wait_ge(sem["mm%d" % k], 1)
-                s.activation(T.yt[:, dst], src, COPY).then_inc(sem["cp%d" % k], 1)
-            g.sync.wait_ge(sem["cp%d" % k], 1)
+            dst = slice(S * o + a, S * o + b)
+            g.sync.wait_ge(sem["y%d" % k], 1)
             g.sync.dma_start(T.y[:, dst], T.yt[:, dst]).then_inc(sem.sty, 16)
-    g.sync.wait_ge(sem.sty, 16 * O * len(PIECES))
+    g.sync.wait_ge(sem.sty, 16 * O * P)

from concourse.bass import DstId, RemoteDMATransfer
from concourse.mybir import dt, ActivationFunctionType

N = 6
XC, CAPP, S, O = 256, 96, 512, 2
K = CAPP // 16
SPLIT = 4
HALF = XC // 2
HV = XC + N * CAPP

PIECES = [128, 192, 192]
VECTOR = [("c", 0), ("c", 1), ("c", 2), ("y", 1, 1), ("y", 2, 0)]
SCALAR = [("s", 0), ("s", 1), ("s", 2), ("y", 0, 0), ("y", 0, 1), ("y", 1, 0), ("y", 2, 1)]
P = len(PIECES)

SCRATCH = {
    "xt": ("sbuf", [128, 4 * XC], "bfloat16"),
    "wt": ("sbuf", [128, O * 512], "bfloat16"),
    "snt": ("sbuf", [128, N * K], "int32"),
    "qlt": ("sbuf", [128, S // 16], "int32"),
    "offs": ("sbuf", [128, N * K], "uint16"),
    "offv": ("sbuf", [128, S // 16], "uint16"),
    "qx": ("sbuf", [128, XC], "float8_e4m3fn_x4"),
    "sx": ("sbuf", [128, XC], "uint8"),
    "qw": ("sbuf", [128, O * 128], "float8_e4m3fn_x4"),
    "sw": ("sbuf", [128, O * 128], "uint8"),
    "qs": ("sbuf", [128, N * CAPP], "float8_e4m3fn_x4"),
    "ss": ("sbuf", [128, N * CAPP], "uint8"),
    "have": ("sbuf", [128, HV], "float8_e4m3fn_x4"),
    "haves": ("sbuf", [128, HV], "uint8"),
    "qv": ("sbuf", [128, S], "float8_e4m3fn_x4"),
    "sv": ("sbuf", [128, S], "uint8"),
    "yt": ("sbuf", [128, O * S], "float32"),
    "acc": ("psum", [128, 512 * O * P], "float32"),
}
SEMAPHORES = ["ldx0", "ldx1", "ldsn", "ldql", "ldw", "offs", "qx", "have", "qw", "offv",
              "arrc", "arrs", "sent", "sty"] + \
             ["pc%d" % i for i in range(N)] + ["ps%d" % i for i in range(N)] + \
             ["c%d" % i for i in range(P)] + ["s%d" % i for i in range(P)] + \
             ["mm%d" % i for i in range(O * P)] + ["y%d" % i for i in range(O * P)]


def bits(engines):
    m = 0
    for e in engines:
        m |= 1 << e
    return m


def near(r, T, topo):
    chip = lambda d: topo.chip(T.cores[d])
    mate = [d for d in range(N) if topo.mates(chip(r), chip(d))][0]
    plane = [d for d in range(N) if d == r or topo.same_plane(chip(r), chip(d))]
    i = plane.index(r)
    return mate, plane[i - 1], plane[(i + 1) % len(plane)]


def calls(r, T, topo):
    mate, prev, nxt = near(r, T, topo)
    far = [near(d, T, topo)[0] for d in (prev, nxt)]
    e = topo.engines(T.cores[r], T.cores[mate])
    two = lambda ds: [(d, e[i::2]) for i, d in enumerate(ds)]
    return [("s", two(far)[:1]), ("s", two(far)[1:]), ("s", two([prev, nxt])),
            ("c", two(far)), ("c", two([prev, nxt])), ("s", [(mate, e)]), ("c", [(mate, e)])]


def run(a):
    return slice(CAPP * a, CAPP * a + CAPP)


def rank_program(g, core, T, topo):
    r = T.rank_of(core)
    if r is None:
        return
    sem = T.sem
    COPY = ActivationFunctionType.Copy
    plan = calls(r, T, topo)

    g.sync.dma_start(T.xt[:, 0:4 * HALF], T.x[:, 0:4 * HALF]).then_inc(sem.ldx0, 16)
    g.scalar.dma_start(T.snt[0:16, :], T.sn[:]).then_inc(sem.ldsn, 16)
    g.sync.dma_start(T.snt[16:32, :], T.sn[:]).then_inc(sem.ldsn, 16)
    g.sync.dma_start(T.xt[:, 4 * HALF:], T.x[:, 4 * HALF:]).then_inc(sem.ldx1, 16)
    g.sync.dma_start(T.qlt[:], T.ql[:]).then_inc(sem.ldql, 16)
    g.sync.dma_start(T.wt[:], T.w[:]).then_inc(sem.ldw, 16)

    scales = [d for kind, to in plan if kind == "s" for d, _ in to]
    first = scales[0]

    def parts(d):
        cuts = (0, SPLIT, K) if d == first else (0, K)
        return [(slice(CAPP * d + 16 * a, CAPP * d + 16 * b), T.offs[:, K * d + a:K * d + b])
                for a, b in zip(cuts, cuts[1:])]

    v, s = g.vector, g.scalar
    v.wait_ge(sem.ldx0, 16)
    v.quantize_mx(T.qx[:, 0:HALF], T.sx[:, 0:HALF], T.xt[:, 0:4 * HALF]).then_inc(sem.qx, 1)
    v.wait_ge(sem.ldsn, 32)
    for u in range(4):
        v.tensor_copy(T.offs[32 * u:32 * u + 32, :], T.snt[0:32, :]).then_inc(sem.offs, 1)
    v.wait_ge(sem.ldx1, 16)
    v.quantize_mx(T.qx[:, HALF:], T.sx[:, HALF:], T.xt[:, 4 * HALF:]).then_inc(sem.qx, 1)
    v.wait_ge(sem.offs, 4)
    v.wait_ge(sem.qx, 2)
    c, o = parts(first)[0]
    v.tensor_copy(T.ss[:, c], T.sx[:].indirect(o)).then_inc(sem["ps%d" % first], 1)
    for d in [d for kind, to in plan if kind == "c" for d, _ in to]:
        for c, o in parts(d):
            v.tensor_copy(T.qs[:, c].bitcast(dt.uint32),
                          T.qx[:].bitcast(dt.uint32).indirect(o)).then_inc(sem["pc%d" % d], 1)
    v.quantize_mx(T.have[:, 0:XC], T.haves[:, 0:XC], T.xt[:]).then_inc(sem.have, 1)
    v.wait_ge(sem.ldql, 16)
    v.tensor_copy(T.offv[:], T.qlt[:]).then_inc(sem.offv, 1)
    v.wait_ge(sem.ldw, 16)
    v.quantize_mx(T.qw[:], T.sw[:], T.wt[:]).then_inc(sem.qw, 1)

    s.wait_ge(sem.offs, 4)
    s.wait_ge(sem.qx, 2)
    for d in scales:
        c, o = parts(d)[-1]
        s.activation(T.ss[:, c], T.sx[:].indirect(o), COPY).then_inc(sem["ps%d" % d], 1)

    here = slice(XC + CAPP * r, XC + CAPP * r + CAPP)
    for kind, to in plan:
        ts = []
        for d, e in to:
            g.wait_ge(sem["p%s%d" % (kind, d)], len(parts(d)))
            if kind == "s":
                out, src, arr = T.haves[:, here], T.ss[:, run(d)], sem.arrs
            else:
                out, src, arr = T.have[:, here].bitcast(dt.uint8), T.qs[:, run(d)].bitcast(dt.uint8), sem.arrc
            rid, pid, _ = topo.addr(T.cores[d])
            if len(to) == 1:
                g.remote_dma(out, src, arr, sem.sent, pid, rid, bits(e))
            ts.append(RemoteDMATransfer(dst_ids=[DstId(rid=rid, pnc=pid)], dma_engine_mask=bits(e),
                                        remote_sem=arr, srcs=[src], dsts=[out]))
        if len(to) > 1:
            g.remote_dma_fused(ts, local_sem=sem.sent)
    g.wait_ge(sem.sent, sum(len(e) for _, to in plan for _, e in to))
    come = {k: sum(len(e) for q in range(N) for kind, to in calls(q, T, topo) for d, e in to if kind == k and d == r)
            for k in "cs"}

    cols = [(sum(PIECES[:i]), sum(PIECES[:i + 1])) for i in range(P)]
    for q, todo in ((v, VECTOR), (s, SCALAR)):
        q.wait_ge(sem.offv, 1)
        q.wait_ge(sem.have, 1)
        seen = set()
        for step in todo:
            kind, i = step[0], step[1]
            a, b = cols[i]
            o = T.offv[:, a // 16:b // 16]
            if kind == "c":
                if kind not in seen:
                    q.wait_ge(sem.arrc, come["c"])
                v.tensor_copy(T.qv[:, a:b].bitcast(dt.uint32),
                              T.have[:].bitcast(dt.uint32).indirect(o)).then_inc(sem["c%d" % i], 1)
            elif kind == "s":
                if kind not in seen:
                    q.wait_ge(sem.arrs, come["s"])
                if q is v:
                    call = v.tensor_copy(T.sv[:, a:b], T.haves[:].indirect(o))
                else:
                    call = s.activation(T.sv[:, a:b], T.haves[:].indirect(o), COPY)
                call.then_inc(sem["s%d" % i], 1)
            else:
                k = O * i + step[2]
                src, dst = T.acc[:, 512 * k:512 * k + b - a], T.yt[:, S * step[2] + a:S * step[2] + b]
                q.wait_ge(sem["mm%d" % k], 1)
                call = v.tensor_copy(dst, src) if q is v else s.activation(dst, src, COPY)
                call.then_inc(sem["y%d" % k], 1)
            seen.add(kind)

    t = g.tensor
    t.wait_ge(sem.qw, 1)
    for i, (a, b) in enumerate(cols):
        t.wait_ge(sem["c%d" % i], 1)
        t.wait_ge(sem["s%d" % i], 1)
        for o in range(O):
            k = O * i + o
            t.matmul_mx(T.acc[:, 512 * k:512 * k + b - a], T.qw[:, 128 * o:128 * o + 128],
                        T.sw[:, 128 * o:128 * o + 128], T.qv[:, a:b], T.sv[:, a:b],
                        True, True).then_inc(sem["mm%d" % k], 1)
            dst = slice(S * o + a, S * o + b)
            g.sync.wait_ge(sem["y%d" % k], 1)
            g.sync.dma_start(T.y[:, dst], T.yt[:, dst]).then_inc(sem.sty, 16)
    g.sync.wait_ge(sem.sty, 16 * O * P)
